import numpy as np
import ml_dtypes


def mxq(x, axis, fmt="e4m3"):
    dtype, down = {"e4m3": (ml_dtypes.float8_e4m3fn, 7), "e5m2": (ml_dtypes.float8_e5m2, 14)}[fmt]
    v = np.moveaxis(np.asarray(x, np.float32).astype(ml_dtypes.bfloat16).astype(np.float64), axis, -1)
    blocks = v.reshape(v.shape[:-1] + (-1, 32))
    amax = np.abs(blocks).max(-1, keepdims=True)
    byte = np.maximum(np.where(amax > 0, np.frexp(amax)[1] - 1 + 127, 0) - down, 1)
    scale = np.exp2(byte - 127.0)
    codes = (blocks / scale).astype(np.float32).astype(dtype).astype(np.float64)
    return np.moveaxis((codes * scale).reshape(v.shape), -1, axis)


WIDE = False


def mx_kscale(k):
    if not WIDE:
        return np.ones(k)
    levels = np.array([10, -10, 5, -5, 0])
    if k % 512:
        return np.exp2(np.random.permutation(np.resize(levels, k // 32))).repeat(32)
    a = np.empty((k // 512, 16))
    for p in range(k // 512):
        a[p, :8] = np.random.permutation(np.resize(levels, 8))
        for g in range(8):
            far = levels[np.abs(levels - a[p, g]) >= 10]
            a[p, g + 8] = far[np.random.randint(len(far))]
    return np.exp2(a.ravel()).repeat(32)


BF16 = ml_dtypes.bfloat16


def bf(x):
    return np.asarray(x, np.float32).astype(BF16)


def f64(x):
    return np.asarray(x).astype(np.float64)


E2M1 = np.array([0.0, 0.5, 1.0, 1.5, 2.0, 3.0, 4.0, 6.0, -0.0, -0.5, -1.0, -1.5, -2.0, -3.0, -4.0, -6.0])


def pack_weight(w, fmt):
    k, n = w.shape
    w = f64(bf(w)).reshape(k // 32, 32, n)
    amax = np.abs(w).max(1)
    if fmt == "e4m3":
        byte = np.frexp(amax)[1] - 1 + 127 - 7
    else:
        mant, ex = np.frexp(amax / 6.0)
        byte = np.where(mant > 0.5, ex, ex - 1) + 127
    byte = np.clip(np.where(amax > 0, byte, 1), 1, 254)
    scaled = (w * np.exp2(127.0 - byte)[:, None, :]).reshape(k, n).astype(np.float32)
    by_word = np.ascontiguousarray(scaled.reshape(k // 512, 128, 4, n).transpose(0, 1, 3, 2))
    if fmt == "e4m3":
        words = by_word.astype(ml_dtypes.float8_e4m3fn).view(np.uint8)
    else:
        c = by_word.astype(ml_dtypes.float4_e2m1fn).view(np.uint8) & 0xF
        words = c[..., 0::2] | (c[..., 1::2] << 4)
    return np.ascontiguousarray(words), np.ascontiguousarray(byte.astype(np.uint8).reshape(k // 512, 16, n))


def unpack_weight(words, scales, fmt):
    g, p, n, _ = words.shape
    if fmt == "e4m3":
        vals = np.ascontiguousarray(words).view(ml_dtypes.float8_e4m3fn).astype(np.float64)
    else:
        nib = np.empty((g, p, n, 4), np.uint8)
        nib[..., 0::2] = words & 0xF
        nib[..., 1::2] = words >> 4
        vals = E2M1[nib]
    vals = vals * np.repeat(np.exp2(scales.astype(np.float64) - 127.0), 8, axis=1)[..., None]
    return vals.transpose(0, 1, 3, 2).reshape(g * 512, n)
def pack4(w):
    words, scales = pack_weight(w, "e2m1")
    return words.reshape(words.shape[0], 128, -1), scales


def unpack4(words, scales):
    return unpack_weight(words.reshape(words.shape[0], 128, -1, 2), scales, "e2m1")


M, D = 1536, 1024


def setup_inputs():
    s, v, r = mx_kscale(D), mx_kscale(D), mx_kscale(D)
    g = np.random.standard_normal((D, D))
    base = (g - g.T) / np.sqrt(2)
    c1 = 0.33 * (base + 0.25 * np.random.standard_normal((D, D))) / np.sqrt(D)
    c2 = 0.33 * (base + 0.25 * np.random.standard_normal((D, D))) / np.sqrt(D)
    c3 = 0.33 * (base + 0.25 * np.random.standard_normal((D, D))) / np.sqrt(D)
    e1_words, e1_scales = pack4(c1 / s[:, None] * v)
    e2_words, e2_scales = pack4(c2 / v[:, None] * r)
    e3_words, e3_scales = pack4(c3 / r[:, None])
    return {"x": bf(np.random.standard_normal((M, D)) * s),
            "a1": bf((0.95 + 0.1 * np.random.standard_normal(D)) * v / s),
            "a2": bf((0.95 + 0.1 * np.random.standard_normal(D)) * r / v),
            "a3": bf((0.95 + 0.1 * np.random.standard_normal(D)) / r),
            "e1_words": e1_words, "e1_scales": e1_scales,
            "e2_words": e2_words, "e2_scales": e2_scales,
            "e3_words": e3_words, "e3_scales": e3_scales}


def reference(x, a1, a2, a3, e1_words, e1_scales, e2_words, e2_scales, e3_words, e3_scales):
    x0 = f64(x)
    x1 = f64(a1) * x0 + (mxq(x0, 1, "e4m3") @ unpack4(e1_words, e1_scales))
    x2 = f64(a2) * x1 + (mxq(x1, 1, "e4m3") @ unpack4(e2_words, e2_scales))
    y = f64(a3) * x2 + (mxq(x2, 1, "e4m3") @ unpack4(e3_words, e3_scales))
    return y

@@ -1,0 +1,256 @@
+from contextlib import ExitStack
+
+import concourse.mybir as mybir
+from concourse.masks import make_identity
+
+M, D = 1536, 1024
+FLOPS = 3 * 2 * M * D * D
+
+F32 = mybir.dt.float32
+BF16 = mybir.dt.bfloat16
+I32 = mybir.dt.int32
+U32 = mybir.dt.uint32
+U8 = mybir.dt.uint8
+FP8X4 = mybir.dt.float8_e4m3fn_x4
+FP4X4 = mybir.dt.float4_e2m1fn_x4
+ALU = mybir.AluOpType
+
+P = 128
+PACK = 4
+HALF = P * PACK
+HALVES = D // HALF
+CHUNK = 512
+CHUNKS = M // CHUNK
+TILES = CHUNK // P
+STAGES = 3
+TURN_AT = {(0, 0): 7, (0, 1): 8, (1, 0): 11, (1, 1): 12, (2, 0): 15, (2, 1): 16}
+
+
+def tile_perturbed_feedback_mixing_t2_kernel(
+    tc, x, a1, a2, a3, e1_words, e1_scales, e2_words, e2_scales, e3_words, e3_scales, out
+):
+    nc = tc.nc
+    gains_in = (a1, a2, a3)
+    words_in = (e1_words, e2_words, e3_words)
+    scales_in = (e1_scales, e2_scales, e3_scales)
+
+    units = sorted(((c, s) for c in range(CHUNKS) for s in range(STAGES)), key=lambda u: (u[0] + u[1], u[1]))
+    steps = [(c, s, h) for (c, s) in units for h in range(HALVES)]
+    first_step = {unit: HALVES * i for i, unit in enumerate(units)}
+
+    with ExitStack() as ctx:
+        keep = ctx.enter_context(tc.tile_pool(name="keep", bufs=1))
+        work = ctx.enter_context(tc.tile_pool(name="work", bufs=2))
+        mx_banks = ctx.enter_context(tc.psum_pool(name="mx_banks", bufs=4))
+        turn_banks = ctx.enter_context(tc.psum_pool(name="turn_banks", bufs=4))
+        ctx.enter_context(tc.manual_schedule())
+
+        identity = keep.tile([P, P], F32, name="identity")
+        make_identity(nc, identity[:])
+
+        gain = []
+        for s in range(STAGES):
+            g_tile = keep.tile([P, HALVES, PACK], BF16, name="gain%d" % s)
+            nc.gpsimd.dma_start(out=g_tile[:], in_=gains_in[s].rearrange("(g p t) -> p g t", g=HALVES, t=PACK))
+            gain.append(g_tile)
+
+        e_words = []
+        e_scales = []
+        for s in range(STAGES):
+            w_tile = keep.tile([P, HALVES, 2 * D], U8, name="e_words%d" % s, align_bytes=64)
+            s_tile = keep.tile([P, HALVES, D], U8, name="e_scales%d" % s, align_bytes=64)
+            nc.vector.memset(s_tile[:].bitcast(I32), 0)
+            e_words.append(w_tile)
+            e_scales.append(s_tile)
+
+        def load_words(s, h):
+            cols = slice(h * 2 * HALF, (h + 1) * 2 * HALF)
+            nc.sync.dma_start(
+                out=e_words[s][:, :, cols].bitcast(I32),
+                in_=words_in[s].rearrange("g p b -> p g b")[:, :, cols].bitcast(I32),
+            )
+
+        def load_scales(s):
+            for q in range(4):
+                nc.sync.dma_start(
+                    out=e_scales[s][32 * q : 32 * q + 4, :, :].bitcast(I32),
+                    in_=scales_in[s][:, 4 * q : 4 * q + 4, :].rearrange("g r n -> r g n").bitcast(I32),
+                )
+
+        x_rows = {}
+
+        def load_x(c, j):
+            rows = work.tile([P, D], BF16, name="x_rows", bufs=8)
+            r0 = c * CHUNK + j * P
+            nc.sync.dma_start(out=rows[:], in_=x[r0 : r0 + P, :])
+            x_rows[c, j] = rows
+
+        sorted_words = {}
+        sorted_scales = {}
+
+        def sort_words(s, h):
+            dst = keep.tile([P, HALVES, 2 * HALF], U8, name="sorted_words%d%d" % (s, h), align_bytes=64)
+            src = e_words[s][:, :, h * 2 * HALF : (h + 1) * 2 * HALF]
+            nc.vector.tensor_copy(
+                out=dst[:].rearrange("p g (t m b) -> p g t m b", t=PACK, b=2),
+                in_=src.rearrange("p g (m t b) -> p g t m b", t=PACK, b=2),
+            )
+            sorted_words[s, h] = dst
+
+        def sort_scales(s, h):
+            dst = keep.tile([P, HALVES, HALF], U8, name="sorted_scales%d%d" % (s, h), align_bytes=64)
+            src = e_scales[s][:, :, h * HALF : (h + 1) * HALF]
+            nc.vector.tensor_copy(
+                out=dst[:].rearrange("p g (t m) -> p g t m", t=PACK),
+                in_=src.rearrange("p g (m t) -> p g t m", t=PACK),
+            )
+            sorted_scales[s, h] = dst
+
+        x_turned = {}
+
+        def turn_x(c, j):
+            if j == 0:
+                x_turned[c] = work.tile([P, HALVES * CHUNK * PACK], BF16, name="x_turned", bufs=3, align_bytes=64)
+            pairs = x_rows[c, j][:].bitcast(F32)
+            bank = turn_banks.tile([P, HALVES, 2, P], F32, name="turn_bank")
+            for g in range(HALVES):
+                for u in range(2):
+                    nc.tensor.transpose(bank[:, g, u, :], pairs[:, 2 * P * g + u : 2 * P * (g + 1) : 2], identity[:])
+            dst = x_turned[c][:].bitcast(F32).rearrange("p (g n u) -> p g n u", g=HALVES, u=2)
+            nc.scalar.copy(out=dst[:, :, j * P : (j + 1) * P, :], in_=bank[:].rearrange("p g u n -> p g n u"))
+
+        codes = {}
+        scales = {}
+
+        def quantize_x(c):
+            c_tile = work.tile([P, HALVES * CHUNK], U32, name="x_codes", bufs=2, align_bytes=64)
+            s_tile = work.tile([P, HALVES * CHUNK], U8, name="x_scales", bufs=2, align_bytes=64)
+            nc.vector.quantize_mx(out=c_tile[:].bitcast(FP8X4), scales=s_tile[:], in_=x_turned[c][:])
+            for g in range(HALVES):
+                codes[c, 0, g] = c_tile[:, g * CHUNK : (g + 1) * CHUNK]
+                scales[c, 0, g] = s_tile[:, g * CHUNK : (g + 1) * CHUNK]
+
+        lines = {}
+        rounded = {}
+        gained = {}
+        kept = {}
+
+        def round_lines(c, s, h):
+            dst = work.tile([P, CHUNK * PACK], BF16, name="rounded", bufs=5, align_bytes=64)
+            nc.scalar.copy(
+                out=dst[:].rearrange("p (n i t) -> p n t i", i=4, t=PACK),
+                in_=lines[c, s, h][:].rearrange("p t (n i) -> p n t i", i=4),
+            )
+            rounded[c, s, h] = dst
+
+        def quantize_lines(c, s, h):
+            c_tile = work.tile([P, CHUNK], U32, name="codes", bufs=6, align_bytes=64)
+            s_tile = work.tile([P, CHUNK], U8, name="scales", bufs=6, align_bytes=64)
+            nc.vector.quantize_mx(out=c_tile[:].bitcast(FP8X4), scales=s_tile[:], in_=rounded[c, s, h][:])
+            codes[c, s + 1, h] = c_tile[:]
+            scales[c, s + 1, h] = s_tile[:]
+
+        def mix_lines(c, s, h):
+            dst = work.tile([P, PACK, CHUNK], F32, name="lines%d" % s, bufs=4 - 2 * s)
+            lines[c, s, h] = dst
+            if s == 1:
+                gained[c, h] = work.tile([P, PACK, CHUNK], F32, name="gained", bufs=3)
+            for t in range(PACK):
+                acc = mx_banks.tile([P, CHUNK], F32, name="acc")
+                for g in range(HALVES):
+                    nc.tensor.matmul_mx(
+                        out=acc[:],
+                        lhsT=sorted_words[s, h][:, g, 2 * P * t : 2 * P * (t + 1)].bitcast(FP4X4),
+                        lhsT_scale=sorted_scales[s, h][:, g, P * t : P * (t + 1)],
+                        rhs=codes[c, s, g].bitcast(FP8X4),
+                        rhs_scale=scales[c, s, g],
+                        start=(g == 0),
+                        stop=(g == HALVES - 1),
+                    )
+                if s == 0:
+                    before = x_turned[c][:].rearrange("p (g n t) -> p g t n", g=HALVES, t=PACK)[:, h, t, :]
+                else:
+                    before = lines[c, s - 1, h][:, t, :]
+                nc.vector.scalar_tensor_tensor(
+                    out=dst[:, t, :], in0=before, scalar=gain[s][:, h, t : t + 1], in1=acc[:],
+                    op0=ALU.mult, op1=ALU.add,
+                )
+                if s == 1:
+                    nc.gpsimd.tensor_scalar(
+                        out=gained[c, h][:, t, :], in0=dst[:, t, :], scalar1=gain[2][:, h, t : t + 1], scalar2=0.0,
+                        op0=ALU.mult, op1=ALU.add,
+                    )
+
+        def turn_gained(c, h):
+            for j in range(TILES):
+                bank = turn_banks.tile([P, PACK, P], F32, name="turn_bank")
+                for t in range(PACK):
+                    nc.tensor.transpose(bank[:, t, :], gained[c, h][:, t, j * P : (j + 1) * P], identity[:])
+                dst = work.tile([P, HALF], F32, name="kept", bufs=16)
+                nc.scalar.copy(out=dst[:].rearrange("f (m t) -> f m t", t=PACK), in_=bank[:].rearrange("f t m -> f m t"))
+                kept[c, h, j] = dst
+
+        def mix_out(c, h):
+            s = STAGES - 1
+            for j in range(TILES):
+                acc = mx_banks.tile([P, HALF], F32, name="acc")
+                for g in range(HALVES):
+                    nc.tensor.matmul_mx(
+                        out=acc[:],
+                        lhsT=codes[c, s, g][:, j * P : (j + 1) * P].bitcast(FP8X4),
+                        lhsT_scale=scales[c, s, g][:, j * P : (j + 1) * P],
+                        rhs=e_words[s][:, g, 2 * HALF * h : 2 * HALF * (h + 1)].bitcast(FP4X4),
+                        rhs_scale=e_scales[s][:, g, HALF * h : HALF * (h + 1)],
+                        start=(g == 0),
+                        stop=(g == HALVES - 1),
+                    )
+                y = kept[c, h, j]
+                nc.vector.tensor_tensor(out=y[:], in0=acc[:], in1=y[:], op=ALU.add)
+                r0 = c * CHUNK + j * P
+                nc.sync.dma_start(out=out[r0 : r0 + P, h * HALF : (h + 1) * HALF], in_=y[:])
+
+        load_words(0, 0)
+        load_words(0, 1)
+        load_scales(0)
+        for c in range(2):
+            for j in range(TILES):
+                load_x(c, j)
+        load_words(1, 0)
+        load_scales(1)
+        load_words(1, 1)
+
+        for h in range(HALVES):
+            sort_words(0, h)
+        for h in range(HALVES):
+            sort_scales(0, h)
+        for j in range(TILES):
+            turn_x(0, j)
+        for j in range(TILES):
+            load_x(2, j)
+        load_words(2, 0)
+        load_words(2, 1)
+        load_scales(2)
+        quantize_x(0)
+
+        x_turn_at = {0: [(1, 0), (1, 1)], 1: [(1, 2), (1, 3)], 3: [(2, 0), (2, 1)], 4: [(2, 2), (2, 3)]}
+        sort_at = {1: [(sort_words, 0)], 2: [(sort_scales, 0)], 3: [(sort_words, 1)], 4: [(sort_scales, 1)]}
+
+        for k, (c, s, h) in enumerate(steps):
+            for cj in x_turn_at.get(k, []):
+                turn_x(*cj)
+            for ch, at in TURN_AT.items():
+                if at == k:
+                    turn_gained(*ch)
+            if k >= 1 and steps[k - 1][1] < STAGES - 1:
+                round_lines(*steps[k - 1])
+            for fn, hh in sort_at.get(k, []):
+                fn(1, hh)
+            for (cc, ss), first in first_step.items():
+                if ss == 0 and cc > 0 and k == first - 1:
+                    quantize_x(cc)
+                if ss > 0 and 0 <= k - (first - HALVES) < HALVES:
+                    quantize_lines(cc, ss - 1, k - (first - HALVES))
+            if s < STAGES - 1:
+                mix_lines(c, s, h)
+            else:
+                mix_out(c, h)

@@ -23,7 +23,7 @@ CHUNK = 512
 CHUNKS = M // CHUNK
 TILES = CHUNK // P
 STAGES = 3
-TURN_AT = {(0, 0): 7, (0, 1): 8, (1, 0): 11, (1, 1): 12, (2, 0): 15, (2, 1): 16}
+TURN_AT = {(0, 0): 7, (0, 1): 8, (1, 0): 11, (1, 1): 12, (2, 0): 15, (2, 1): 17}
 
 
 def tile_perturbed_feedback_mixing_t2_kernel(
@@ -79,11 +79,38 @@ def tile_perturbed_feedback_mixing_t2_kernel(
 
         x_rows = {}
 
-        def load_x(c, j):
-            rows = work.tile([P, D], BF16, name="x_rows", bufs=8)
+        def load_x(c, j, n=1):
+            rows = work.tile([P, n * D], BF16, name="x_rows%d" % n, bufs=6 if n == 1 else 1)
             r0 = c * CHUNK + j * P
-            nc.sync.dma_start(out=rows[:], in_=x[r0 : r0 + P, :])
-            x_rows[c, j] = rows
+            nc.sync.dma_start(
+                out=rows[:].rearrange("p (j d) -> p j d", j=n),
+                in_=x[r0 : r0 + n * P, :].rearrange("(j p) d -> p j d", j=n),
+            )
+            for i in range(n):
+                x_rows[c, j + i] = rows[:, i * D : (i + 1) * D]
+
+        def warm_operand():
+            zeros = keep.tile([P, PACK * P], BF16, name="zeros", align_bytes=64)
+            nc.vector.memset(zeros[:].bitcast(I32), 0)
+            c_tile = keep.tile([P, P], U32, name="warm_codes", align_bytes=64)
+            s_tile = keep.tile([P, P], U8, name="warm_scales", align_bytes=64)
+            nc.vector.quantize_mx(out=c_tile[:].bitcast(FP8X4), scales=s_tile[:], in_=zeros[:])
+            return c_tile, s_tile
+
+        warm_codes, warm_scales = warm_operand()
+
+        def warm_up(n):
+            acc = mx_banks.tile([P, HALF], F32, name="acc")
+            for i in range(n):
+                nc.tensor.matmul_mx(
+                    out=acc[:],
+                    lhsT=warm_codes[:].bitcast(FP8X4),
+                    lhsT_scale=warm_scales[:],
+                    rhs=e_words[0][:, 0, 0 : 2 * HALF].bitcast(FP4X4),
+                    rhs_scale=e_scales[0][:, 0, 0:HALF],
+                    start=True,
+                    stop=True,
+                )
 
         sorted_words = {}
         sorted_scales = {}
@@ -107,15 +134,27 @@ def tile_perturbed_feedback_mixing_t2_kernel(
             sorted_scales[s, h] = dst
 
         x_turned = {}
+        x_pairs = {}
+
+        def sort_x(c, j):
+            dst = work.tile([P, HALVES, 2, P], F32, name="x_pairs", bufs=8)
+            nc.scalar.copy(
+                out=dst[:], in_=x_rows[c, j].bitcast(F32).rearrange("f (g m u) -> f g u m", g=HALVES, u=2)
+            )
+            x_pairs[c, j] = dst
 
         def turn_x(c, j):
             if j == 0:
                 x_turned[c] = work.tile([P, HALVES * CHUNK * PACK], BF16, name="x_turned", bufs=3, align_bytes=64)
-            pairs = x_rows[c, j][:].bitcast(F32)
+            pairs = x_rows[c, j].bitcast(F32)
             bank = turn_banks.tile([P, HALVES, 2, P], F32, name="turn_bank")
             for g in range(HALVES):
                 for u in range(2):
-                    nc.tensor.transpose(bank[:, g, u, :], pairs[:, 2 * P * g + u : 2 * P * (g + 1) : 2], identity[:])
+                    if (c, j) in x_pairs:
+                        src = x_pairs[c, j][:, g, u, :]
+                    else:
+                        src = pairs[:, 2 * P * g + u : 2 * P * (g + 1) : 2]
+                    nc.tensor.transpose(bank[:, g, u, :], src, identity[:])
             dst = x_turned[c][:].bitcast(F32).rearrange("p (g n u) -> p g n u", g=HALVES, u=2)
             nc.scalar.copy(out=dst[:, :, j * P : (j + 1) * P, :], in_=bank[:].rearrange("p g u n -> p g n u"))
 
@@ -136,7 +175,7 @@ def tile_perturbed_feedback_mixing_t2_kernel(
         kept = {}
 
         def round_lines(c, s, h):
-            dst = work.tile([P, CHUNK * PACK], BF16, name="rounded", bufs=5, align_bytes=64)
+            dst = work.tile([P, CHUNK * PACK], BF16, name="rounded", bufs=6, align_bytes=64)
             nc.scalar.copy(
                 out=dst[:].rearrange("p (n i t) -> p n t i", i=4, t=PACK),
                 in_=lines[c, s, h][:].rearrange("p t (n i) -> p n t i", i=4),
@@ -150,12 +189,13 @@ def tile_perturbed_feedback_mixing_t2_kernel(
             codes[c, s + 1, h] = c_tile[:]
             scales[c, s + 1, h] = s_tile[:]
 
-        def mix_lines(c, s, h):
+        def mix_lines(c, s, h, between):
             dst = work.tile([P, PACK, CHUNK], F32, name="lines%d" % s, bufs=4 - 2 * s)
             lines[c, s, h] = dst
             if s == 1:
-                gained[c, h] = work.tile([P, PACK, CHUNK], F32, name="gained", bufs=3)
+                gained[c, h] = work.tile([P, PACK, CHUNK], F32, name="gained", bufs=2)
             for t in range(PACK):
+                between(t)
                 acc = mx_banks.tile([P, CHUNK], F32, name="acc")
                 for g in range(HALVES):
                     nc.tensor.matmul_mx(
@@ -186,13 +226,14 @@ def tile_perturbed_feedback_mixing_t2_kernel(
                 bank = turn_banks.tile([P, PACK, P], F32, name="turn_bank")
                 for t in range(PACK):
                     nc.tensor.transpose(bank[:, t, :], gained[c, h][:, t, j * P : (j + 1) * P], identity[:])
-                dst = work.tile([P, HALF], F32, name="kept", bufs=16)
+                dst = work.tile([P, HALF], F32, name="kept", bufs=12)
                 nc.scalar.copy(out=dst[:].rearrange("f (m t) -> f m t", t=PACK), in_=bank[:].rearrange("f t m -> f m t"))
                 kept[c, h, j] = dst
 
-        def mix_out(c, h):
+        def mix_out(c, h, between):
             s = STAGES - 1
             for j in range(TILES):
+                between(j)
                 acc = mx_banks.tile([P, HALF], F32, name="acc")
                 for g in range(HALVES):
                     nc.tensor.matmul_mx(
@@ -210,30 +251,46 @@ def tile_perturbed_feedback_mixing_t2_kernel(
                 nc.sync.dma_start(out=out[r0 : r0 + P, h * HALF : (h + 1) * HALF], in_=y[:])
 
         load_words(0, 0)
-        load_words(0, 1)
+        load_x(0, 0)
+        load_x(0, 1)
         load_scales(0)
-        for c in range(2):
-            for j in range(TILES):
-                load_x(c, j)
+        load_x(0, 2, 2)
+        load_words(0, 1)
         load_words(1, 0)
-        load_scales(1)
+        load_x(1, 0)
+        load_x(1, 1)
+        load_x(1, 2)
+        load_x(1, 3)
         load_words(1, 1)
+        load_scales(1)
 
-        for h in range(HALVES):
-            sort_words(0, h)
-        for h in range(HALVES):
-            sort_scales(0, h)
+        sort_words(0, 0)
+        sort_scales(0, 0)
+        sort_scales(0, 1)
+        sort_words(0, 1)
+        turn_x(0, 0)
+        turn_x(0, 1)
+        turn_x(0, 2)
+        turn_x(0, 3)
         for j in range(TILES):
-            turn_x(0, j)
+            sort_x(1, j)
         for j in range(TILES):
             load_x(2, j)
         load_words(2, 0)
         load_words(2, 1)
         load_scales(2)
         quantize_x(0)
+        warm_up(4)
 
-        x_turn_at = {0: [(1, 0), (1, 1)], 1: [(1, 2), (1, 3)], 3: [(2, 0), (2, 1)], 4: [(2, 2), (2, 3)]}
-        sort_at = {1: [(sort_words, 0)], 2: [(sort_scales, 0)], 3: [(sort_words, 1)], 4: [(sort_scales, 1)]}
+        x_turn_at = {1: [(1, 0), (1, 1), (1, 2), (1, 3)], 2: [(2, 0), (2, 1)], 3: [(2, 2), (2, 3)]}
+        fill_at = {(0, 0): [(sort_words, (1, 0))], (1, 0): [(sort_words, (1, 1)), (sort_scales, (1, 0)), (sort_scales, (1, 1))]}
+        quantize_at = {
+            (1, 0): [(1, -1, 0)],
+            (2, 0): [(0, 0, 0)], (3, 0): [(0, 0, 1)], (4, 0): [(2, -1, 0)],
+            (7, 0): [(1, 0, 0), (1, 0, 1)], (8, 0): [(0, 1, 0), (0, 1, 1)],
+            (11, 0): [(2, 0, 0), (2, 0, 1)], (12, 0): [(1, 1, 0), (1, 1, 1)],
+            (15, 0): [(2, 1, 0), (2, 1, 1)],
+        }
 
         for k, (c, s, h) in enumerate(steps):
             for cj in x_turn_at.get(k, []):
@@ -243,14 +300,17 @@ def tile_perturbed_feedback_mixing_t2_kernel(
                     turn_gained(*ch)
             if k >= 1 and steps[k - 1][1] < STAGES - 1:
                 round_lines(*steps[k - 1])
-            for fn, hh in sort_at.get(k, []):
-                fn(1, hh)
-            for (cc, ss), first in first_step.items():
-                if ss == 0 and cc > 0 and k == first - 1:
-                    quantize_x(cc)
-                if ss > 0 and 0 <= k - (first - HALVES) < HALVES:
-                    quantize_lines(cc, ss - 1, k - (first - HALVES))
+
+            def between(i):
+                for fn, args in fill_at.get((k, i), []):
+                    fn(*args)
+                for (cc, ss, hh) in quantize_at.get((k, i), []):
+                    if ss < 0:
+                        quantize_x(cc)
+                    else:
+                        quantize_lines(cc, ss, hh)
+
             if s < STAGES - 1:
-                mix_lines(c, s, h)
+                mix_lines(c, s, h, between)
             else:
-                mix_out(c, h)
+                mix_out(c, h, between)

@@ -14,6 +14,12 @@ U8 = mybir.dt.uint8
 FP8X4 = mybir.dt.float8_e4m3fn_x4
 FP4X4 = mybir.dt.float4_e2m1fn_x4
 ALU = mybir.AluOpType
+ACT = mybir.ActivationFunctionType
+POOL_FRAMES = 256
+RUN = 4
+VECTOR_ROUNDS = [(2,1,1)]
+POOL_ROUNDS = [(2,1,1)] + [(0,0,0),(0,0,1),(1,0,0),(2,0,0),(2,0,1)]
+WARM = 4
 
 P = 128
 PACK = 4
@@ -23,7 +29,7 @@ CHUNK = 512
 CHUNKS = M // CHUNK
 TILES = CHUNK // P
 STAGES = 3
-TURN_AT = {(0, 0): 7, (0, 1): 8, (1, 0): 11, (1, 1): 12, (2, 0): 15, (2, 1): 17}
+TURN_AT = {(0, 0): 7, (0, 1): 9, (1, 0): 11, (1, 1): 13, (2, 0): 15, (2, 1): 17}
 
 
 def tile_perturbed_feedback_mixing_t2_kernel(
@@ -45,28 +51,29 @@ def tile_perturbed_feedback_mixing_t2_kernel(
         turn_banks = ctx.enter_context(tc.psum_pool(name="turn_banks", bufs=4))
         ctx.enter_context(tc.manual_schedule())
 
-        identity = keep.tile([P, P], F32, name="identity")
-        make_identity(nc, identity[:])
-
         gain = []
         for s in range(STAGES):
             g_tile = keep.tile([P, HALVES, PACK], BF16, name="gain%d" % s)
-            nc.gpsimd.dma_start(out=g_tile[:], in_=gains_in[s].rearrange("(g p t) -> p g t", g=HALVES, t=PACK))
             gain.append(g_tile)
 
-        e_words = []
+        e_words = {}
         e_scales = []
         for s in range(STAGES):
-            w_tile = keep.tile([P, HALVES, 2 * D], U8, name="e_words%d" % s, align_bytes=64)
             s_tile = keep.tile([P, HALVES, D], U8, name="e_scales%d" % s, align_bytes=64)
-            nc.vector.memset(s_tile[:].bitcast(I32), 0)
-            e_words.append(w_tile)
+            (nc.gpsimd if s == 0 else nc.vector).memset(s_tile[:].bitcast(I32), 0)
             e_scales.append(s_tile)
+
+        identity = keep.tile([P, P], F32, name="identity")
+        make_identity(nc, identity[:])
+
+        def load_gain(s):
+            nc.sync.dma_start(out=gain[s][:], in_=gains_in[s].rearrange("(g p t) -> p g t", g=HALVES, t=PACK))
 
         def load_words(s, h):
             cols = slice(h * 2 * HALF, (h + 1) * 2 * HALF)
+            e_words[s, h] = keep.tile([P, HALVES, 2 * HALF], U8, name="e_words%d%d" % (s, h), align_bytes=64)
             nc.sync.dma_start(
-                out=e_words[s][:, :, cols].bitcast(I32),
+                out=e_words[s, h][:].bitcast(I32),
                 in_=words_in[s].rearrange("g p b -> p g b")[:, :, cols].bitcast(I32),
             )
 
@@ -80,7 +87,7 @@ def tile_perturbed_feedback_mixing_t2_kernel(
         x_rows = {}
 
         def load_x(c, j, n=1):
-            rows = work.tile([P, n * D], BF16, name="x_rows%d" % n, bufs=6 if n == 1 else 1)
+            rows = work.tile([P, n * D], BF16, name="x_rows%d" % n, bufs=8 if n == 1 else 1)
             r0 = c * CHUNK + j * P
             nc.sync.dma_start(
                 out=rows[:].rearrange("p (j d) -> p j d", j=n),
@@ -106,7 +113,7 @@ def tile_perturbed_feedback_mixing_t2_kernel(
                     out=acc[:],
                     lhsT=warm_codes[:].bitcast(FP8X4),
                     lhsT_scale=warm_scales[:],
-                    rhs=e_words[0][:, 0, 0 : 2 * HALF].bitcast(FP4X4),
+                    rhs=e_words[0, 0][:, 0, :].bitcast(FP4X4),
                     rhs_scale=e_scales[0][:, 0, 0:HALF],
                     start=True,
                     stop=True,
@@ -117,31 +124,22 @@ def tile_perturbed_feedback_mixing_t2_kernel(
 
         def sort_words(s, h):
             dst = keep.tile([P, HALVES, 2 * HALF], U8, name="sorted_words%d%d" % (s, h), align_bytes=64)
-            src = e_words[s][:, :, h * 2 * HALF : (h + 1) * 2 * HALF]
+            src = e_words[s, h][:]
             nc.vector.tensor_copy(
                 out=dst[:].rearrange("p g (t m b) -> p g t m b", t=PACK, b=2),
                 in_=src.rearrange("p g (m t b) -> p g t m b", t=PACK, b=2),
             )
             sorted_words[s, h] = dst
 
-        def sort_scales(s, h):
-            dst = keep.tile([P, HALVES, HALF], U8, name="sorted_scales%d%d" % (s, h), align_bytes=64)
-            src = e_scales[s][:, :, h * HALF : (h + 1) * HALF]
+        def sort_scales(s):
+            dst = keep.tile([P, HALVES * HALVES, HALF], U8, name="sorted_scales%d" % s, align_bytes=64)
             nc.vector.tensor_copy(
-                out=dst[:].rearrange("p g (t m) -> p g t m", t=PACK),
-                in_=src.rearrange("p g (m t) -> p g t m", t=PACK),
+                out=dst[:].rearrange("p a (t m) -> p a t m", t=PACK),
+                in_=e_scales[s][:].rearrange("p g (h m t) -> p (g h) t m", h=HALVES, t=PACK),
             )
-            sorted_scales[s, h] = dst
+            sorted_scales[s] = dst
 
         x_turned = {}
-        x_pairs = {}
-
-        def sort_x(c, j):
-            dst = work.tile([P, HALVES, 2, P], F32, name="x_pairs", bufs=8)
-            nc.scalar.copy(
-                out=dst[:], in_=x_rows[c, j].bitcast(F32).rearrange("f (g m u) -> f g u m", g=HALVES, u=2)
-            )
-            x_pairs[c, j] = dst
 
         def turn_x(c, j):
             if j == 0:
@@ -150,10 +148,7 @@ def tile_perturbed_feedback_mixing_t2_kernel(
             bank = turn_banks.tile([P, HALVES, 2, P], F32, name="turn_bank")
             for g in range(HALVES):
                 for u in range(2):
-                    if (c, j) in x_pairs:
-                        src = x_pairs[c, j][:, g, u, :]
-                    else:
-                        src = pairs[:, 2 * P * g + u : 2 * P * (g + 1) : 2]
+                    src = pairs[:, 2 * P * g + u : 2 * P * (g + 1) : 2]
                     nc.tensor.transpose(bank[:, g, u, :], src, identity[:])
             dst = x_turned[c][:].bitcast(F32).rearrange("p (g n u) -> p g n u", g=HALVES, u=2)
             nc.scalar.copy(out=dst[:, :, j * P : (j + 1) * P, :], in_=bank[:].rearrange("p g u n -> p g n u"))
@@ -161,33 +156,45 @@ def tile_perturbed_feedback_mixing_t2_kernel(
         codes = {}
         scales = {}
 
-        def quantize_x(c):
-            c_tile = work.tile([P, HALVES * CHUNK], U32, name="x_codes", bufs=2, align_bytes=64)
-            s_tile = work.tile([P, HALVES * CHUNK], U8, name="x_scales", bufs=2, align_bytes=64)
-            nc.vector.quantize_mx(out=c_tile[:].bitcast(FP8X4), scales=s_tile[:], in_=x_turned[c][:])
-            for g in range(HALVES):
-                codes[c, 0, g] = c_tile[:, g * CHUNK : (g + 1) * CHUNK]
-                scales[c, 0, g] = s_tile[:, g * CHUNK : (g + 1) * CHUNK]
-
         lines = {}
         rounded = {}
         gained = {}
         kept = {}
 
         def round_lines(c, s, h):
-            dst = work.tile([P, CHUNK * PACK], BF16, name="rounded", bufs=6, align_bytes=64)
+            if h == 0:
+                rounded[c, s] = work.tile([P, HALVES * CHUNK * PACK], BF16, name="rounded", bufs=3, align_bytes=64)
+            dst = rounded[c, s][:, h * CHUNK * PACK : (h + 1) * CHUNK * PACK]
+            src = lines[c, s, h]
+            cut = CHUNK - POOL_FRAMES if (c, s, h) in POOL_ROUNDS else CHUNK
             nc.scalar.copy(
-                out=dst[:].rearrange("p (n i t) -> p n t i", i=4, t=PACK),
-                in_=lines[c, s, h][:].rearrange("p t (n i) -> p n t i", i=4),
+                out=dst[:, : cut * PACK].rearrange("p (n i t) -> p n t i", i=4, t=PACK),
+                in_=src[:, :, :cut].rearrange("p t (n i) -> p n t i", i=4),
             )
-            rounded[c, s, h] = dst
+            if cut == CHUNK or (c, s, h) in VECTOR_ROUNDS:
+                return
+            nc.gpsimd.tensor_scalar(
+                out=dst[:, cut * PACK :].rearrange("p (n t) -> p n t", t=PACK),
+                in0=src[:, :, cut:].rearrange("p t n -> p n t"),
+                scalar1=1.0, scalar2=0.0, op0=ALU.mult, op1=ALU.add,
+            )
 
-        def quantize_lines(c, s, h):
-            c_tile = work.tile([P, CHUNK], U32, name="codes", bufs=6, align_bytes=64)
-            s_tile = work.tile([P, CHUNK], U8, name="scales", bufs=6, align_bytes=64)
-            nc.vector.quantize_mx(out=c_tile[:].bitcast(FP8X4), scales=s_tile[:], in_=rounded[c, s, h][:])
-            codes[c, s + 1, h] = c_tile[:]
-            scales[c, s + 1, h] = s_tile[:]
+        def round_rest(c, s, h):
+            cut = CHUNK - POOL_FRAMES
+            dst = rounded[c, s][:, h * CHUNK * PACK : (h + 1) * CHUNK * PACK]
+            nc.vector.tensor_copy(
+                out=dst[:, cut * PACK :].rearrange("p (n i t) -> p n t i", i=4, t=PACK),
+                in_=lines[c, s, h][:, :, cut:].rearrange("p t (n i) -> p n t i", i=4),
+            )
+
+        def quantize(c, s):
+            src = x_turned[c] if s == 0 else rounded[c, s - 1]
+            c_tile = work.tile([P, HALVES * CHUNK], U32, name="codes", bufs=4, align_bytes=64)
+            s_tile = work.tile([P, HALVES * CHUNK], U8, name="scales", bufs=4, align_bytes=64)
+            nc.vector.quantize_mx(out=c_tile[:].bitcast(FP8X4), scales=s_tile[:], in_=src[:])
+            for g in range(HALVES):
+                codes[c, s, g] = c_tile[:, g * CHUNK : (g + 1) * CHUNK]
+                scales[c, s, g] = s_tile[:, g * CHUNK : (g + 1) * CHUNK]
 
         def mix_lines(c, s, h, between):
             dst = work.tile([P, PACK, CHUNK], F32, name="lines%d" % s, bufs=4 - 2 * s)
@@ -201,7 +208,7 @@ def tile_perturbed_feedback_mixing_t2_kernel(
                     nc.tensor.matmul_mx(
                         out=acc[:],
                         lhsT=sorted_words[s, h][:, g, 2 * P * t : 2 * P * (t + 1)].bitcast(FP4X4),
-                        lhsT_scale=sorted_scales[s, h][:, g, P * t : P * (t + 1)],
+                        lhsT_scale=sorted_scales[s][:, HALVES * g + h, P * t : P * (t + 1)],
                         rhs=codes[c, s, g].bitcast(FP8X4),
                         rhs_scale=scales[c, s, g],
                         start=(g == 0),
@@ -221,8 +228,8 @@ def tile_perturbed_feedback_mixing_t2_kernel(
                         op0=ALU.mult, op1=ALU.add,
                     )
 
-        def turn_gained(c, h):
-            for j in range(TILES):
+        def turn_gained(c, h, js):
+            for j in js:
                 bank = turn_banks.tile([P, PACK, P], F32, name="turn_bank")
                 for t in range(PACK):
                     nc.tensor.transpose(bank[:, t, :], gained[c, h][:, t, j * P : (j + 1) * P], identity[:])
@@ -240,7 +247,7 @@ def tile_perturbed_feedback_mixing_t2_kernel(
                         out=acc[:],
                         lhsT=codes[c, s, g][:, j * P : (j + 1) * P].bitcast(FP8X4),
                         lhsT_scale=scales[c, s, g][:, j * P : (j + 1) * P],
-                        rhs=e_words[s][:, g, 2 * HALF * h : 2 * HALF * (h + 1)].bitcast(FP4X4),
+                        rhs=e_words[s, h][:, g, :].bitcast(FP4X4),
                         rhs_scale=e_scales[s][:, g, HALF * h : HALF * (h + 1)],
                         start=(g == 0),
                         stop=(g == HALVES - 1),
@@ -251,64 +258,52 @@ def tile_perturbed_feedback_mixing_t2_kernel(
                 nc.sync.dma_start(out=out[r0 : r0 + P, h * HALF : (h + 1) * HALF], in_=y[:])
 
         load_words(0, 0)
+        load_scales(0)
         load_x(0, 0)
         load_x(0, 1)
-        load_scales(0)
         load_x(0, 2, 2)
         load_words(0, 1)
         load_words(1, 0)
-        load_x(1, 0)
-        load_x(1, 1)
-        load_x(1, 2)
-        load_x(1, 3)
-        load_words(1, 1)
+        load_gain(0)
         load_scales(1)
+        load_words(1, 1)
+        for j in range(TILES):
+            load_x(1, j)
+        load_gain(1)
+        load_gain(2)
 
         sort_words(0, 0)
-        sort_scales(0, 0)
-        sort_scales(0, 1)
+        sort_scales(0)
         sort_words(0, 1)
-        turn_x(0, 0)
-        turn_x(0, 1)
-        turn_x(0, 2)
-        turn_x(0, 3)
         for j in range(TILES):
-            sort_x(1, j)
+            turn_x(0, j)
         for j in range(TILES):
             load_x(2, j)
         load_words(2, 0)
         load_words(2, 1)
         load_scales(2)
-        quantize_x(0)
-        warm_up(4)
+        quantize(0, 0)
+        warm_up(WARM)
 
-        x_turn_at = {1: [(1, 0), (1, 1), (1, 2), (1, 3)], 2: [(2, 0), (2, 1)], 3: [(2, 2), (2, 3)]}
-        fill_at = {(0, 0): [(sort_words, (1, 0))], (1, 0): [(sort_words, (1, 1)), (sort_scales, (1, 0)), (sort_scales, (1, 1))]}
-        quantize_at = {
-            (1, 0): [(1, -1, 0)],
-            (2, 0): [(0, 0, 0)], (3, 0): [(0, 0, 1)], (4, 0): [(2, -1, 0)],
-            (7, 0): [(1, 0, 0), (1, 0, 1)], (8, 0): [(0, 1, 0), (0, 1, 1)],
-            (11, 0): [(2, 0, 0), (2, 0, 1)], (12, 0): [(1, 1, 0), (1, 1, 1)],
-            (15, 0): [(2, 1, 0), (2, 1, 1)],
+        fill_at = {(14, 2): [(round_rest, (2, 1, 1))], (0, 0): [(sort_words, (1, 0))], (0, 2): [(sort_words, (1, 1))], (0, 3): [(sort_scales, (1,))]}
+        turn_at = {
+            (0, 2): [(turn_x, (1, 0)), (turn_x, (1, 1))], (1, 0): [(turn_x, (1, 2)), (turn_x, (1, 3))],
+            (2, 0): [(turn_x, (2, 0)), (turn_x, (2, 1))], (3, 0): [(turn_x, (2, 2)), (turn_x, (2, 3))],
         }
+        for (c, h), at in TURN_AT.items():
+            for j in range(0, TILES, RUN):
+                turn_at[at, j] = [(turn_gained, (c, h, range(j, j + RUN)))]
+        quantize_at = {1: (1, 0), 3: (0, 1), 4: (2, 0), 7: (1, 1), 8: (0, 2), 11: (2, 1), 12: (1, 2), 15: (2, 2)}
 
         for k, (c, s, h) in enumerate(steps):
-            for cj in x_turn_at.get(k, []):
-                turn_x(*cj)
-            for ch, at in TURN_AT.items():
-                if at == k:
-                    turn_gained(*ch)
-            if k >= 1 and steps[k - 1][1] < STAGES - 1:
-                round_lines(*steps[k - 1])
 
             def between(i):
-                for fn, args in fill_at.get((k, i), []):
+                for fn, args in turn_at.get((k, i), []) + fill_at.get((k, i), []):
                     fn(*args)
-                for (cc, ss, hh) in quantize_at.get((k, i), []):
-                    if ss < 0:
-                        quantize_x(cc)
-                    else:
-                        quantize_lines(cc, ss, hh)
+                if i == 0 and k >= 1 and steps[k - 1][1] < STAGES - 1:
+                    round_lines(*steps[k - 1])
+                if i == 0 and k in quantize_at:
+                    quantize(*quantize_at[k])
 
             if s < STAGES - 1:
                 mix_lines(c, s, h, between)

@@ -4,7 +4,8 @@ import concourse.mybir as mybir
 from concourse.masks import make_identity
 
 M, D = 1536, 1024
-FLOPS = 3 * 2 * M * D * D
+MIXES = 3
+FLOPS = MIXES * 2 * M * D * D
 
 F32 = mybir.dt.float32
 BF16 = mybir.dt.bfloat16
@@ -14,22 +15,23 @@ U8 = mybir.dt.uint8
 FP8X4 = mybir.dt.float8_e4m3fn_x4
 FP4X4 = mybir.dt.float4_e2m1fn_x4
 ALU = mybir.AluOpType
-ACT = mybir.ActivationFunctionType
-POOL_FRAMES = 256
-RUN = 4
-VECTOR_ROUNDS = [(2,1,1)]
-POOL_ROUNDS = [(2,1,1)] + [(0,0,0),(0,0,1),(1,0,0),(2,0,0),(2,0,1)]
-WARM = 4
 
 P = 128
-PACK = 4
-HALF = P * PACK
+SLOTS = 4
+HALF = P * SLOTS
 HALVES = D // HALF
 CHUNK = 512
 CHUNKS = M // CHUNK
 TILES = CHUNK // P
-STAGES = 3
-TURN_AT = {(0, 0): 7, (0, 1): 9, (1, 0): 11, (1, 1): 13, (2, 0): 15, (2, 1): 17}
+QUADRANTS = 4
+RUN = 4
+GAIN_MIX = 1
+LAST_MIX = MIXES - 1
+
+GPSIMD_FRAMES = 192
+GPSIMD_FIRST_FRAMES = 16
+VECTOR_FRAMES = 256
+TURN_LAG = 3
 
 
 def tile_perturbed_feedback_mixing_t2_kernel(
@@ -40,272 +42,273 @@ def tile_perturbed_feedback_mixing_t2_kernel(
     words_in = (e1_words, e2_words, e3_words)
     scales_in = (e1_scales, e2_scales, e3_scales)
 
-    units = sorted(((c, s) for c in range(CHUNKS) for s in range(STAGES)), key=lambda u: (u[0] + u[1], u[1]))
-    steps = [(c, s, h) for (c, s) in units for h in range(HALVES)]
-    first_step = {unit: HALVES * i for i, unit in enumerate(units)}
+    pairs = sorted(((c, s) for c in range(CHUNKS) for s in range(MIXES)), key=lambda cs: (cs[0] + cs[1], cs[1]))
+    steps = [(c, s, h) for (c, s) in pairs for h in range(HALVES)]
 
     with ExitStack() as ctx:
         keep = ctx.enter_context(tc.tile_pool(name="keep", bufs=1))
-        work = ctx.enter_context(tc.tile_pool(name="work", bufs=2))
+        work = ctx.enter_context(tc.tile_pool(name="work", bufs=3))
         mx_banks = ctx.enter_context(tc.psum_pool(name="mx_banks", bufs=4))
         turn_banks = ctx.enter_context(tc.psum_pool(name="turn_banks", bufs=4))
         ctx.enter_context(tc.manual_schedule())
 
-        gain = []
-        for s in range(STAGES):
-            g_tile = keep.tile([P, HALVES, PACK], BF16, name="gain%d" % s)
-            gain.append(g_tile)
-
-        e_words = {}
         e_scales = []
-        for s in range(STAGES):
-            s_tile = keep.tile([P, HALVES, D], U8, name="e_scales%d" % s, align_bytes=64)
-            (nc.gpsimd if s == 0 else nc.vector).memset(s_tile[:].bitcast(I32), 0)
-            e_scales.append(s_tile)
+        for s in range(MIXES):
+            scale_tile = keep.tile([P, HALVES, D], U8, name="e_scales%d" % s, align_bytes=64)
+            (nc.gpsimd if s == 0 else nc.vector).memset(scale_tile[:].bitcast(I32), 0)
+            e_scales.append(scale_tile)
 
         identity = keep.tile([P, P], F32, name="identity")
         make_identity(nc, identity[:])
 
+        gain = {}
+        e_words = {}
+        x_rows = {}
+        sorted_words = {}
+        sorted_scales = {}
+        x_turned = {}
+        lines = {}
+        rounded = {}
+        codes = {}
+        scales = {}
+        gained = {}
+        turned = {}
+
         def load_gain(s):
-            nc.sync.dma_start(out=gain[s][:], in_=gains_in[s].rearrange("(g p t) -> p g t", g=HALVES, t=PACK))
+            gain[s] = keep.tile([P, HALVES, SLOTS], BF16, name="gain%d" % s)
+            nc.sync.dma_start(out=gain[s][:], in_=gains_in[s].rearrange("(h p t) -> p h t", h=HALVES, t=SLOTS))
 
         def load_words(s, h):
-            cols = slice(h * 2 * HALF, (h + 1) * 2 * HALF)
             e_words[s, h] = keep.tile([P, HALVES, 2 * HALF], U8, name="e_words%d%d" % (s, h), align_bytes=64)
             nc.sync.dma_start(
                 out=e_words[s, h][:].bitcast(I32),
-                in_=words_in[s].rearrange("g p b -> p g b")[:, :, cols].bitcast(I32),
+                in_=words_in[s].rearrange("g p b -> p g b")[:, :, 2 * HALF * h : 2 * HALF * (h + 1)].bitcast(I32),
             )
 
         def load_scales(s):
-            for q in range(4):
+            for quad in range(QUADRANTS):
                 nc.sync.dma_start(
-                    out=e_scales[s][32 * q : 32 * q + 4, :, :].bitcast(I32),
-                    in_=scales_in[s][:, 4 * q : 4 * q + 4, :].rearrange("g r n -> r g n").bitcast(I32),
+                    out=e_scales[s][32 * quad : 32 * quad + 4, :, :].bitcast(I32),
+                    in_=scales_in[s][:, 4 * quad : 4 * quad + 4, :].rearrange("g r n -> r g n").bitcast(I32),
                 )
 
-        x_rows = {}
+        def load_x(c):
+            for j in range(TILES):
+                x_rows[c, j] = work.tile([P, D], BF16, name="x_rows", bufs=2 * TILES)
+                row = c * CHUNK + j * P
+                nc.sync.dma_start(out=x_rows[c, j][:], in_=x[row : row + P, :])
 
-        def load_x(c, j, n=1):
-            rows = work.tile([P, n * D], BF16, name="x_rows%d" % n, bufs=8 if n == 1 else 1)
-            r0 = c * CHUNK + j * P
-            nc.sync.dma_start(
-                out=rows[:].rearrange("p (j d) -> p j d", j=n),
-                in_=x[r0 : r0 + n * P, :].rearrange("(j p) d -> p j d", j=n),
+        def sort_words(s, h, engine):
+            sorted_words[s, h] = keep.tile([P, HALVES, 2 * HALF], U8, name="sorted_words%d%d" % (s, h), align_bytes=64)
+            engine.tensor_copy(
+                out=sorted_words[s, h][:].rearrange("p g (t m b) -> p g t m b", t=SLOTS, b=2),
+                in_=e_words[s, h][:].rearrange("p g (m t b) -> p g t m b", t=SLOTS, b=2),
             )
-            for i in range(n):
-                x_rows[c, j + i] = rows[:, i * D : (i + 1) * D]
-
-        def warm_operand():
-            zeros = keep.tile([P, PACK * P], BF16, name="zeros", align_bytes=64)
-            nc.vector.memset(zeros[:].bitcast(I32), 0)
-            c_tile = keep.tile([P, P], U32, name="warm_codes", align_bytes=64)
-            s_tile = keep.tile([P, P], U8, name="warm_scales", align_bytes=64)
-            nc.vector.quantize_mx(out=c_tile[:].bitcast(FP8X4), scales=s_tile[:], in_=zeros[:])
-            return c_tile, s_tile
-
-        warm_codes, warm_scales = warm_operand()
-
-        def warm_up(n):
-            acc = mx_banks.tile([P, HALF], F32, name="acc")
-            for i in range(n):
-                nc.tensor.matmul_mx(
-                    out=acc[:],
-                    lhsT=warm_codes[:].bitcast(FP8X4),
-                    lhsT_scale=warm_scales[:],
-                    rhs=e_words[0, 0][:, 0, :].bitcast(FP4X4),
-                    rhs_scale=e_scales[0][:, 0, 0:HALF],
-                    start=True,
-                    stop=True,
-                )
-
-        sorted_words = {}
-        sorted_scales = {}
-
-        def sort_words(s, h):
-            dst = keep.tile([P, HALVES, 2 * HALF], U8, name="sorted_words%d%d" % (s, h), align_bytes=64)
-            src = e_words[s, h][:]
-            nc.vector.tensor_copy(
-                out=dst[:].rearrange("p g (t m b) -> p g t m b", t=PACK, b=2),
-                in_=src.rearrange("p g (m t b) -> p g t m b", t=PACK, b=2),
-            )
-            sorted_words[s, h] = dst
 
         def sort_scales(s):
-            dst = keep.tile([P, HALVES * HALVES, HALF], U8, name="sorted_scales%d" % s, align_bytes=64)
+            sorted_scales[s] = keep.tile([P, HALVES * HALVES, HALF], U8, name="sorted_scales%d" % s, align_bytes=64)
             nc.vector.tensor_copy(
-                out=dst[:].rearrange("p a (t m) -> p a t m", t=PACK),
-                in_=e_scales[s][:].rearrange("p g (h m t) -> p (g h) t m", h=HALVES, t=PACK),
+                out=sorted_scales[s][:].rearrange("p a (t m) -> p a t m", t=SLOTS),
+                in_=e_scales[s][:].rearrange("p g (h m t) -> p (g h) t m", h=HALVES, t=SLOTS),
             )
-            sorted_scales[s] = dst
 
-        x_turned = {}
+        def turn_x(c, tiles):
+            for j in tiles:
+                if j == 0:
+                    x_turned[c] = work.tile([P, HALVES * CHUNK * SLOTS], BF16, name="x_turned", align_bytes=64)
+                line_pairs = x_rows[c, j][:].bitcast(F32)
+                bank = turn_banks.tile([P, HALVES, 2, P], F32, name="turn_bank")
+                for g in range(HALVES):
+                    for u in range(2):
+                        nc.tensor.transpose(
+                            bank[:, g, u, :], line_pairs[:, 2 * P * g + u : 2 * P * (g + 1) : 2], identity[:]
+                        )
+                as_pairs = x_turned[c][:].bitcast(F32).rearrange("p (g n u) -> p g n u", g=HALVES, u=2)
+                nc.scalar.copy(out=as_pairs[:, :, j * P : (j + 1) * P, :], in_=bank[:].rearrange("p g u n -> p g n u"))
 
-        def turn_x(c, j):
-            if j == 0:
-                x_turned[c] = work.tile([P, HALVES * CHUNK * PACK], BF16, name="x_turned", bufs=3, align_bytes=64)
-            pairs = x_rows[c, j].bitcast(F32)
-            bank = turn_banks.tile([P, HALVES, 2, P], F32, name="turn_bank")
-            for g in range(HALVES):
-                for u in range(2):
-                    src = pairs[:, 2 * P * g + u : 2 * P * (g + 1) : 2]
-                    nc.tensor.transpose(bank[:, g, u, :], src, identity[:])
-            dst = x_turned[c][:].bitcast(F32).rearrange("p (g n u) -> p g n u", g=HALVES, u=2)
-            nc.scalar.copy(out=dst[:, :, j * P : (j + 1) * P, :], in_=bank[:].rearrange("p g u n -> p g n u"))
+        def rounding_views(step, frames):
+            c, s, h = step
+            first = h * CHUNK + frames.start
+            last = h * CHUNK + frames.stop
+            return rounded[c, s][:, SLOTS * first : SLOTS * last], lines[step][:, :, frames]
 
-        codes = {}
-        scales = {}
-
-        lines = {}
-        rounded = {}
-        gained = {}
-        kept = {}
-
-        def round_lines(c, s, h):
-            if h == 0:
-                rounded[c, s] = work.tile([P, HALVES * CHUNK * PACK], BF16, name="rounded", bufs=3, align_bytes=64)
-            dst = rounded[c, s][:, h * CHUNK * PACK : (h + 1) * CHUNK * PACK]
-            src = lines[c, s, h]
-            cut = CHUNK - POOL_FRAMES if (c, s, h) in POOL_ROUNDS else CHUNK
-            nc.scalar.copy(
-                out=dst[:, : cut * PACK].rearrange("p (n i t) -> p n t i", i=4, t=PACK),
-                in_=src[:, :, :cut].rearrange("p t (n i) -> p n t i", i=4),
+        def round_by_copy(copy, step, frames):
+            dst, src = rounding_views(step, frames)
+            copy(
+                out=dst.rearrange("p (n i t) -> p n t i", i=RUN, t=SLOTS),
+                in_=src.rearrange("p t (n i) -> p n t i", i=RUN),
             )
-            if cut == CHUNK or (c, s, h) in VECTOR_ROUNDS:
-                return
+
+        def round_on_gpsimd(step, frames):
+            dst, src = rounding_views(step, frames)
             nc.gpsimd.tensor_scalar(
-                out=dst[:, cut * PACK :].rearrange("p (n t) -> p n t", t=PACK),
-                in0=src[:, :, cut:].rearrange("p t n -> p n t"),
-                scalar1=1.0, scalar2=0.0, op0=ALU.mult, op1=ALU.add,
+                out=dst.rearrange("p (n t) -> p n t", t=SLOTS),
+                in0=src.rearrange("p t n -> p n t"),
+                scalar1=1.0,
+                scalar2=0.0,
+                op0=ALU.mult,
+                op1=ALU.add,
             )
 
-        def round_rest(c, s, h):
-            cut = CHUNK - POOL_FRAMES
-            dst = rounded[c, s][:, h * CHUNK * PACK : (h + 1) * CHUNK * PACK]
-            nc.vector.tensor_copy(
-                out=dst[:, cut * PACK :].rearrange("p (n i t) -> p n t i", i=4, t=PACK),
-                in_=lines[c, s, h][:, :, cut:].rearrange("p t (n i) -> p n t i", i=4),
-            )
+        def round_lines(step, gpsimd_frames, vector_frames):
+            c, s, h = step
+            if h == 0:
+                rounded[c, s] = work.tile([P, HALVES * CHUNK * SLOTS], BF16, name="rounded", align_bytes=64)
+            round_by_copy(nc.scalar.copy, step, slice(0, CHUNK - gpsimd_frames - vector_frames))
+            if gpsimd_frames:
+                round_on_gpsimd(step, slice(CHUNK - gpsimd_frames, CHUNK))
 
-        def quantize(c, s):
+        def quantize(c, s, calls):
             src = x_turned[c] if s == 0 else rounded[c, s - 1]
-            c_tile = work.tile([P, HALVES * CHUNK], U32, name="codes", bufs=4, align_bytes=64)
-            s_tile = work.tile([P, HALVES * CHUNK], U8, name="scales", bufs=4, align_bytes=64)
-            nc.vector.quantize_mx(out=c_tile[:].bitcast(FP8X4), scales=s_tile[:], in_=src[:])
-            for g in range(HALVES):
-                codes[c, s, g] = c_tile[:, g * CHUNK : (g + 1) * CHUNK]
-                scales[c, s, g] = s_tile[:, g * CHUNK : (g + 1) * CHUNK]
-
-        def mix_lines(c, s, h, between):
-            dst = work.tile([P, PACK, CHUNK], F32, name="lines%d" % s, bufs=4 - 2 * s)
-            lines[c, s, h] = dst
-            if s == 1:
-                gained[c, h] = work.tile([P, PACK, CHUNK], F32, name="gained", bufs=2)
-            for t in range(PACK):
-                between(t)
-                acc = mx_banks.tile([P, CHUNK], F32, name="acc")
-                for g in range(HALVES):
-                    nc.tensor.matmul_mx(
-                        out=acc[:],
-                        lhsT=sorted_words[s, h][:, g, 2 * P * t : 2 * P * (t + 1)].bitcast(FP4X4),
-                        lhsT_scale=sorted_scales[s][:, HALVES * g + h, P * t : P * (t + 1)],
-                        rhs=codes[c, s, g].bitcast(FP8X4),
-                        rhs_scale=scales[c, s, g],
-                        start=(g == 0),
-                        stop=(g == HALVES - 1),
-                    )
-                if s == 0:
-                    before = x_turned[c][:].rearrange("p (g n t) -> p g t n", g=HALVES, t=PACK)[:, h, t, :]
-                else:
-                    before = lines[c, s - 1, h][:, t, :]
-                nc.vector.scalar_tensor_tensor(
-                    out=dst[:, t, :], in0=before, scalar=gain[s][:, h, t : t + 1], in1=acc[:],
-                    op0=ALU.mult, op1=ALU.add,
+            code_tile = work.tile([P, HALVES * CHUNK], U32, name="codes", bufs=4, align_bytes=64)
+            scale_tile = work.tile([P, HALVES * CHUNK], U8, name="scales", bufs=4, align_bytes=64)
+            width = HALVES * CHUNK // calls
+            for i in range(calls):
+                nc.vector.quantize_mx(
+                    out=code_tile[:, i * width : (i + 1) * width].bitcast(FP8X4),
+                    scales=scale_tile[:, i * width : (i + 1) * width],
+                    in_=src[:, SLOTS * i * width : SLOTS * (i + 1) * width],
                 )
-                if s == 1:
-                    nc.gpsimd.tensor_scalar(
-                        out=gained[c, h][:, t, :], in0=dst[:, t, :], scalar1=gain[2][:, h, t : t + 1], scalar2=0.0,
-                        op0=ALU.mult, op1=ALU.add,
-                    )
+            for g in range(HALVES):
+                codes[c, s, g] = code_tile[:, g * CHUNK : (g + 1) * CHUNK]
+                scales[c, s, g] = scale_tile[:, g * CHUNK : (g + 1) * CHUNK]
 
-        def turn_gained(c, h, js):
-            for j in js:
-                bank = turn_banks.tile([P, PACK, P], F32, name="turn_bank")
-                for t in range(PACK):
-                    nc.tensor.transpose(bank[:, t, :], gained[c, h][:, t, j * P : (j + 1) * P], identity[:])
-                dst = work.tile([P, HALF], F32, name="kept", bufs=12)
-                nc.scalar.copy(out=dst[:].rearrange("f (m t) -> f m t", t=PACK), in_=bank[:].rearrange("f t m -> f m t"))
-                kept[c, h, j] = dst
-
-        def mix_out(c, h, between):
-            s = STAGES - 1
+        def turn_gained(c, h):
             for j in range(TILES):
-                between(j)
-                acc = mx_banks.tile([P, HALF], F32, name="acc")
-                for g in range(HALVES):
-                    nc.tensor.matmul_mx(
-                        out=acc[:],
-                        lhsT=codes[c, s, g][:, j * P : (j + 1) * P].bitcast(FP8X4),
-                        lhsT_scale=scales[c, s, g][:, j * P : (j + 1) * P],
-                        rhs=e_words[s, h][:, g, :].bitcast(FP4X4),
-                        rhs_scale=e_scales[s][:, g, HALF * h : HALF * (h + 1)],
-                        start=(g == 0),
-                        stop=(g == HALVES - 1),
-                    )
-                y = kept[c, h, j]
-                nc.vector.tensor_tensor(out=y[:], in0=acc[:], in1=y[:], op=ALU.add)
-                r0 = c * CHUNK + j * P
-                nc.sync.dma_start(out=out[r0 : r0 + P, h * HALF : (h + 1) * HALF], in_=y[:])
+                bank = turn_banks.tile([P, SLOTS, P], F32, name="turn_bank")
+                for t in range(SLOTS):
+                    nc.tensor.transpose(bank[:, t, :], gained[c, h][:, t, j * P : (j + 1) * P], identity[:])
+                turned[c, h, j] = work.tile([P, HALF], F32, name="turned", bufs=4 * TILES)
+                nc.scalar.copy(
+                    out=turned[c, h, j][:].rearrange("f (m t) -> f m t", t=SLOTS),
+                    in_=bank[:].rearrange("f t m -> f m t"),
+                )
+
+        def mix_lines(step, t):
+            c, s, h = step
+            if t == 0:
+                lines[step] = work.tile([P, SLOTS, CHUNK], F32, name="lines%d" % s, bufs=4 - s)
+                if s == GAIN_MIX:
+                    gained[c, h] = work.tile([P, SLOTS, CHUNK], F32, name="gained")
+            product = mx_banks.tile([P, CHUNK], F32, name="product")
+            for g in range(HALVES):
+                nc.tensor.matmul_mx(
+                    out=product[:],
+                    lhsT=sorted_words[s, h][:, g, 2 * P * t : 2 * P * (t + 1)].bitcast(FP4X4),
+                    lhsT_scale=sorted_scales[s][:, HALVES * g + h, P * t : P * (t + 1)],
+                    rhs=codes[c, s, g].bitcast(FP8X4),
+                    rhs_scale=scales[c, s, g],
+                    start=(g == 0),
+                    stop=(g == HALVES - 1),
+                )
+            if s == 0:
+                own = x_turned[c][:].rearrange("p (h n t) -> p h t n", h=HALVES, t=SLOTS)[:, h, t, :]
+            else:
+                own = lines[c, s - 1, h][:, t, :]
+            nc.vector.scalar_tensor_tensor(
+                out=lines[step][:, t, :],
+                in0=own,
+                scalar=gain[s][:, h, t : t + 1],
+                in1=product[:],
+                op0=ALU.mult,
+                op1=ALU.add,
+            )
+            if s == GAIN_MIX:
+                nc.gpsimd.tensor_scalar(
+                    out=gained[c, h][:, t, :],
+                    in0=lines[step][:, t, :],
+                    scalar1=gain[LAST_MIX][:, h, t : t + 1],
+                    scalar2=0.0,
+                    op0=ALU.mult,
+                    op1=ALU.add,
+                )
+
+        def mix_out(step, j):
+            c, s, h = step
+            product = mx_banks.tile([P, HALF], F32, name="product")
+            for g in range(HALVES):
+                nc.tensor.matmul_mx(
+                    out=product[:],
+                    lhsT=codes[c, s, g][:, j * P : (j + 1) * P].bitcast(FP8X4),
+                    lhsT_scale=scales[c, s, g][:, j * P : (j + 1) * P],
+                    rhs=e_words[s, h][:, g, :].bitcast(FP4X4),
+                    rhs_scale=e_scales[s][:, g, HALF * h : HALF * (h + 1)],
+                    start=(g == 0),
+                    stop=(g == HALVES - 1),
+                )
+            y = turned[c, h, j]
+            nc.vector.tensor_tensor(out=y[:], in0=product[:], in1=y[:], op=ALU.add)
+            row = c * CHUNK + j * P
+            nc.sync.dma_start(out=out[row : row + P, h * HALF : (h + 1) * HALF], in_=y[:])
+
+        before = {}
+
+        def put(k, i, call, *args):
+            before.setdefault((k, i), []).append((call, args))
+
+        first_half, second_half = range(TILES // 2), range(TILES // 2, TILES)
+        middle, last_bank = TILES // 2, TILES - 1
+
+        put(0, middle, turn_x, 1, second_half)
+        second_mix_starts = steps.index((0, 1, 0))
+        put(second_mix_starts - 1, 0, turn_x, 2, first_half)
+        put(second_mix_starts - 1, middle, turn_x, 2, second_half)
+        gain_steps = [step for step in steps if step[1] == GAIN_MIX]
+        for n, (c, s, h) in enumerate(gain_steps):
+            put(second_mix_starts + TURN_LAG + 2 * n, 0, turn_gained, c, h)
+        turning_steps = set(k for (k, i) in before if i == 0)
+
+        put(0, 0, sort_words, 0, 1, nc.vector)
+        put(0, middle, sort_scales, 1)
+        put(2, last_bank, sort_words, 1, 1, nc.vector)
+
+        rounded_steps = [step for step in steps if step[1] != LAST_MIX]
+        for step in rounded_steps:
+            k = steps.index(step) + 1
+            if step == rounded_steps[0]:
+                put(k, 0, round_lines, step, GPSIMD_FIRST_FRAMES, 0)
+                put(k, 0, sort_words, 1, 0, nc.gpsimd)
+            elif step == rounded_steps[-1]:
+                put(k, 0, round_lines, step, 0, VECTOR_FRAMES)
+                put(k, middle, round_by_copy, nc.vector.tensor_copy, step, slice(CHUNK - VECTOR_FRAMES, CHUNK))
+            elif k in turning_steps and step[1] != GAIN_MIX:
+                put(k, 0, round_lines, step, GPSIMD_FRAMES, 0)
+            else:
+                put(k, 0, round_lines, step, 0, 0)
+
+        for c, s in pairs[1:]:
+            k = steps.index((c, s, 0)) - 1
+            if steps[k - 1][1] == GAIN_MIX:
+                k = k - 1
+            put(k, 0, quantize, c, s, 1)
 
         load_words(0, 0)
         load_scales(0)
-        load_x(0, 0)
-        load_x(0, 1)
-        load_x(0, 2, 2)
+        load_x(0)
         load_words(0, 1)
-        load_words(1, 0)
         load_gain(0)
+        load_x(1)
+        load_words(1, 0)
         load_scales(1)
         load_words(1, 1)
-        for j in range(TILES):
-            load_x(1, j)
         load_gain(1)
         load_gain(2)
 
-        sort_words(0, 0)
+        sort_words(0, 0, nc.vector)
         sort_scales(0)
-        sort_words(0, 1)
-        for j in range(TILES):
-            turn_x(0, j)
-        for j in range(TILES):
-            load_x(2, j)
+        turn_x(0, range(TILES))
+        turn_x(1, first_half)
+        load_x(2)
         load_words(2, 0)
         load_words(2, 1)
         load_scales(2)
-        quantize(0, 0)
-        warm_up(WARM)
+        quantize(0, 0, HALVES)
 
-        fill_at = {(14, 2): [(round_rest, (2, 1, 1))], (0, 0): [(sort_words, (1, 0))], (0, 2): [(sort_words, (1, 1))], (0, 3): [(sort_scales, (1,))]}
-        turn_at = {
-            (0, 2): [(turn_x, (1, 0)), (turn_x, (1, 1))], (1, 0): [(turn_x, (1, 2)), (turn_x, (1, 3))],
-            (2, 0): [(turn_x, (2, 0)), (turn_x, (2, 1))], (3, 0): [(turn_x, (2, 2)), (turn_x, (2, 3))],
-        }
-        for (c, h), at in TURN_AT.items():
-            for j in range(0, TILES, RUN):
-                turn_at[at, j] = [(turn_gained, (c, h, range(j, j + RUN)))]
-        quantize_at = {1: (1, 0), 3: (0, 1), 4: (2, 0), 7: (1, 1), 8: (0, 2), 11: (2, 1), 12: (1, 2), 15: (2, 2)}
-
-        for k, (c, s, h) in enumerate(steps):
-
-            def between(i):
-                for fn, args in turn_at.get((k, i), []) + fill_at.get((k, i), []):
-                    fn(*args)
-                if i == 0 and k >= 1 and steps[k - 1][1] < STAGES - 1:
-                    round_lines(*steps[k - 1])
-                if i == 0 and k in quantize_at:
-                    quantize(*quantize_at[k])
-
-            if s < STAGES - 1:
-                mix_lines(c, s, h, between)
-            else:
-                mix_out(c, h, between)
+        for k, step in enumerate(steps):
+            for i in range(TILES):
+                for call, args in before.get((k, i), []):
+                    call(*args)
+                if step[1] == LAST_MIX:
+                    mix_out(step, i)
+                else:
+                    mix_lines(step, i)

from contextlib import ExitStack

import concourse.mybir as mybir
from concourse.masks import make_identity

M, D = 1536, 1024
MIXES = 3
FLOPS = MIXES * 2 * M * D * D

F32 = mybir.dt.float32
BF16 = mybir.dt.bfloat16
I32 = mybir.dt.int32
U32 = mybir.dt.uint32
U8 = mybir.dt.uint8
FP8X4 = mybir.dt.float8_e4m3fn_x4
FP4X4 = mybir.dt.float4_e2m1fn_x4
ALU = mybir.AluOpType

P = 128
SLOTS = 4
HALF = P * SLOTS
HALVES = D // HALF
CHUNK = 512
CHUNKS = M // CHUNK
TILES = CHUNK // P
QUADRANTS = 4
RUN = 4
GAIN_MIX = 1
LAST_MIX = MIXES - 1

GPSIMD_FRAMES = 192
GPSIMD_FIRST_FRAMES = 16
VECTOR_FRAMES = 256
TURN_LAG = 3


def tile_perturbed_feedback_mixing_t2_kernel(
    tc, x, a1, a2, a3, e1_words, e1_scales, e2_words, e2_scales, e3_words, e3_scales, out
):
    nc = tc.nc
    gains_in = (a1, a2, a3)
    words_in = (e1_words, e2_words, e3_words)
    scales_in = (e1_scales, e2_scales, e3_scales)

    pairs = sorted(((c, s) for c in range(CHUNKS) for s in range(MIXES)), key=lambda cs: (cs[0] + cs[1], cs[1]))
    steps = [(c, s, h) for (c, s) in pairs for h in range(HALVES)]

    with ExitStack() as ctx:
        keep = ctx.enter_context(tc.tile_pool(name="keep", bufs=1))
        work = ctx.enter_context(tc.tile_pool(name="work", bufs=3))
        mx_banks = ctx.enter_context(tc.psum_pool(name="mx_banks", bufs=4))
        turn_banks = ctx.enter_context(tc.psum_pool(name="turn_banks", bufs=4))
        ctx.enter_context(tc.manual_schedule())

        e_scales = []
        for s in range(MIXES):
            scale_tile = keep.tile([P, HALVES, D], U8, name="e_scales%d" % s, align_bytes=64)
            (nc.gpsimd if s == 0 else nc.vector).memset(scale_tile[:].bitcast(I32), 0)
            e_scales.append(scale_tile)

        identity = keep.tile([P, P], F32, name="identity")
        make_identity(nc, identity[:])

        gain = {}
        e_words = {}
        x_rows = {}
        sorted_words = {}
        sorted_scales = {}
        x_turned = {}
        lines = {}
        rounded = {}
        codes = {}
        scales = {}
        gained = {}
        turned = {}

        def load_gain(s):
            gain[s] = keep.tile([P, HALVES, SLOTS], BF16, name="gain%d" % s)
            nc.sync.dma_start(out=gain[s][:], in_=gains_in[s].rearrange("(h p t) -> p h t", h=HALVES, t=SLOTS))

        def load_words(s, h):
            e_words[s, h] = keep.tile([P, HALVES, 2 * HALF], U8, name="e_words%d%d" % (s, h), align_bytes=64)
            nc.sync.dma_start(
                out=e_words[s, h][:].bitcast(I32),
                in_=words_in[s].rearrange("g p b -> p g b")[:, :, 2 * HALF * h : 2 * HALF * (h + 1)].bitcast(I32),
            )

        def load_scales(s):
            for quad in range(QUADRANTS):
                nc.sync.dma_start(
                    out=e_scales[s][32 * quad : 32 * quad + 4, :, :].bitcast(I32),
                    in_=scales_in[s][:, 4 * quad : 4 * quad + 4, :].rearrange("g r n -> r g n").bitcast(I32),
                )

        def load_x(c):
            for j in range(TILES):
                x_rows[c, j] = work.tile([P, D], BF16, name="x_rows", bufs=2 * TILES)
                row = c * CHUNK + j * P
                nc.sync.dma_start(out=x_rows[c, j][:], in_=x[row : row + P, :])

        def sort_words(s, h, engine):
            sorted_words[s, h] = keep.tile([P, HALVES, 2 * HALF], U8, name="sorted_words%d%d" % (s, h), align_bytes=64)
            engine.tensor_copy(
                out=sorted_words[s, h][:].rearrange("p g (t m b) -> p g t m b", t=SLOTS, b=2),
                in_=e_words[s, h][:].rearrange("p g (m t b) -> p g t m b", t=SLOTS, b=2),
            )

        def sort_scales(s):
            sorted_scales[s] = keep.tile([P, HALVES * HALVES, HALF], U8, name="sorted_scales%d" % s, align_bytes=64)
            nc.vector.tensor_copy(
                out=sorted_scales[s][:].rearrange("p a (t m) -> p a t m", t=SLOTS),
                in_=e_scales[s][:].rearrange("p g (h m t) -> p (g h) t m", h=HALVES, t=SLOTS),
            )

        def turn_x(c, tiles):
            for j in tiles:
                if j == 0:
                    x_turned[c] = work.tile([P, HALVES * CHUNK * SLOTS], BF16, name="x_turned", align_bytes=64)
                line_pairs = x_rows[c, j][:].bitcast(F32)
                bank = turn_banks.tile([P, HALVES, 2, P], F32, name="turn_bank")
                for g in range(HALVES):
                    for u in range(2):
                        nc.tensor.transpose(
                            bank[:, g, u, :], line_pairs[:, 2 * P * g + u : 2 * P * (g + 1) : 2], identity[:]
                        )
                as_pairs = x_turned[c][:].bitcast(F32).rearrange("p (g n u) -> p g n u", g=HALVES, u=2)
                nc.scalar.copy(out=as_pairs[:, :, j * P : (j + 1) * P, :], in_=bank[:].rearrange("p g u n -> p g n u"))

        def rounding_views(step, frames):
            c, s, h = step
            first = h * CHUNK + frames.start
            last = h * CHUNK + frames.stop
            return rounded[c, s][:, SLOTS * first : SLOTS * last], lines[step][:, :, frames]

        def round_by_copy(copy, step, frames):
            dst, src = rounding_views(step, frames)
            copy(
                out=dst.rearrange("p (n i t) -> p n t i", i=RUN, t=SLOTS),
                in_=src.rearrange("p t (n i) -> p n t i", i=RUN),
            )

        def round_on_gpsimd(step, frames):
            dst, src = rounding_views(step, frames)
            nc.gpsimd.tensor_scalar(
                out=dst.rearrange("p (n t) -> p n t", t=SLOTS),
                in0=src.rearrange("p t n -> p n t"),
                scalar1=1.0,
                scalar2=0.0,
                op0=ALU.mult,
                op1=ALU.add,
            )

        def round_lines(step, gpsimd_frames, vector_frames):
            c, s, h = step
            if h == 0:
                rounded[c, s] = work.tile([P, HALVES * CHUNK * SLOTS], BF16, name="rounded", align_bytes=64)
            round_by_copy(nc.scalar.copy, step, slice(0, CHUNK - gpsimd_frames - vector_frames))
            if gpsimd_frames:
                round_on_gpsimd(step, slice(CHUNK - gpsimd_frames, CHUNK))

        def quantize(c, s, calls):
            src = x_turned[c] if s == 0 else rounded[c, s - 1]
            code_tile = work.tile([P, HALVES * CHUNK], U32, name="codes", bufs=4, align_bytes=64)
            scale_tile = work.tile([P, HALVES * CHUNK], U8, name="scales", bufs=4, align_bytes=64)
            width = HALVES * CHUNK // calls
            for i in range(calls):
                nc.vector.quantize_mx(
                    out=code_tile[:, i * width : (i + 1) * width].bitcast(FP8X4),
                    scales=scale_tile[:, i * width : (i + 1) * width],
                    in_=src[:, SLOTS * i * width : SLOTS * (i + 1) * width],
                )
            for g in range(HALVES):
                codes[c, s, g] = code_tile[:, g * CHUNK : (g + 1) * CHUNK]
                scales[c, s, g] = scale_tile[:, g * CHUNK : (g + 1) * CHUNK]

        def turn_gained(c, h):
            for j in range(TILES):
                bank = turn_banks.tile([P, SLOTS, P], F32, name="turn_bank")
                for t in range(SLOTS):
                    nc.tensor.transpose(bank[:, t, :], gained[c, h][:, t, j * P : (j + 1) * P], identity[:])
                turned[c, h, j] = work.tile([P, HALF], F32, name="turned", bufs=4 * TILES)
                nc.scalar.copy(
                    out=turned[c, h, j][:].rearrange("f (m t) -> f m t", t=SLOTS),
                    in_=bank[:].rearrange("f t m -> f m t"),
                )

        def mix_lines(step, t):
            c, s, h = step
            if t == 0:
                lines[step] = work.tile([P, SLOTS, CHUNK], F32, name="lines%d" % s, bufs=4 - s)
                if s == GAIN_MIX:
                    gained[c, h] = work.tile([P, SLOTS, CHUNK], F32, name="gained")
            product = mx_banks.tile([P, CHUNK], F32, name="product")
            for g in range(HALVES):
                nc.tensor.matmul_mx(
                    out=product[:],
                    lhsT=sorted_words[s, h][:, g, 2 * P * t : 2 * P * (t + 1)].bitcast(FP4X4),
                    lhsT_scale=sorted_scales[s][:, HALVES * g + h, P * t : P * (t + 1)],
                    rhs=codes[c, s, g].bitcast(FP8X4),
                    rhs_scale=scales[c, s, g],
                    start=(g == 0),
                    stop=(g == HALVES - 1),
                )
            if s == 0:
                own = x_turned[c][:].rearrange("p (h n t) -> p h t n", h=HALVES, t=SLOTS)[:, h, t, :]
            else:
                own = lines[c, s - 1, h][:, t, :]
            nc.vector.scalar_tensor_tensor(
                out=lines[step][:, t, :],
                in0=own,
                scalar=gain[s][:, h, t : t + 1],
                in1=product[:],
                op0=ALU.mult,
                op1=ALU.add,
            )
            if s == GAIN_MIX:
                nc.gpsimd.tensor_scalar(
                    out=gained[c, h][:, t, :],
                    in0=lines[step][:, t, :],
                    scalar1=gain[LAST_MIX][:, h, t : t + 1],
                    scalar2=0.0,
                    op0=ALU.mult,
                    op1=ALU.add,
                )

        def mix_out(step, j):
            c, s, h = step
            product = mx_banks.tile([P, HALF], F32, name="product")
            for g in range(HALVES):
                nc.tensor.matmul_mx(
                    out=product[:],
                    lhsT=codes[c, s, g][:, j * P : (j + 1) * P].bitcast(FP8X4),
                    lhsT_scale=scales[c, s, g][:, j * P : (j + 1) * P],
                    rhs=e_words[s, h][:, g, :].bitcast(FP4X4),
                    rhs_scale=e_scales[s][:, g, HALF * h : HALF * (h + 1)],
                    start=(g == 0),
                    stop=(g == HALVES - 1),
                )
            y = turned[c, h, j]
            nc.vector.tensor_tensor(out=y[:], in0=product[:], in1=y[:], op=ALU.add)
            row = c * CHUNK + j * P
            nc.sync.dma_start(out=out[row : row + P, h * HALF : (h + 1) * HALF], in_=y[:])

        before = {}

        def put(k, i, call, *args):
            before.setdefault((k, i), []).append((call, args))

        first_half, second_half = range(TILES // 2), range(TILES // 2, TILES)
        middle, last_bank = TILES // 2, TILES - 1

        put(0, middle, turn_x, 1, second_half)
        second_mix_starts = steps.index((0, 1, 0))
        put(second_mix_starts - 1, 0, turn_x, 2, first_half)
        put(second_mix_starts - 1, middle, turn_x, 2, second_half)
        gain_steps = [step for step in steps if step[1] == GAIN_MIX]
        for n, (c, s, h) in enumerate(gain_steps):
            put(second_mix_starts + TURN_LAG + 2 * n, 0, turn_gained, c, h)
        turning_steps = set(k for (k, i) in before if i == 0)

        put(0, 0, sort_words, 0, 1, nc.vector)
        put(0, middle, sort_scales, 1)
        put(2, last_bank, sort_words, 1, 1, nc.vector)

        rounded_steps = [step for step in steps if step[1] != LAST_MIX]
        for step in rounded_steps:
            k = steps.index(step) + 1
            if step == rounded_steps[0]:
                put(k, 0, round_lines, step, GPSIMD_FIRST_FRAMES, 0)
                put(k, 0, sort_words, 1, 0, nc.gpsimd)
            elif step == rounded_steps[-1]:
                put(k, 0, round_lines, step, 0, VECTOR_FRAMES)
                put(k, middle, round_by_copy, nc.vector.tensor_copy, step, slice(CHUNK - VECTOR_FRAMES, CHUNK))
            elif k in turning_steps and step[1] != GAIN_MIX:
                put(k, 0, round_lines, step, GPSIMD_FRAMES, 0)
            else:
                put(k, 0, round_lines, step, 0, 0)

        for c, s in pairs[1:]:
            k = steps.index((c, s, 0)) - 1
            if steps[k - 1][1] == GAIN_MIX:
                k = k - 1
            put(k, 0, quantize, c, s, 1)

        load_words(0, 0)
        load_scales(0)
        load_x(0)
        load_words(0, 1)
        load_gain(0)
        load_x(1)
        load_words(1, 0)
        load_scales(1)
        load_words(1, 1)
        load_gain(1)
        load_gain(2)

        sort_words(0, 0, nc.vector)
        sort_scales(0)
        turn_x(0, range(TILES))
        turn_x(1, first_half)
        load_x(2)
        load_words(2, 0)
        load_words(2, 1)
        load_scales(2)
        quantize(0, 0, HALVES)

        for k, step in enumerate(steps):
            for i in range(TILES):
                for call, args in before.get((k, i), []):
                    call(*args)
                if step[1] == LAST_MIX:
                    mix_out(step, i)
                else:
                    mix_lines(step, i)
